import numpy as np
import ml_dtypes


def mxq(x, axis, fmt="e4m3"):
    dtype, down = {"e4m3": (ml_dtypes.float8_e4m3fn, 7), "e5m2": (ml_dtypes.float8_e5m2, 14)}[fmt]
    v = np.moveaxis(np.asarray(x, np.float32).astype(ml_dtypes.bfloat16).astype(np.float64), axis, -1)
    blocks = v.reshape(v.shape[:-1] + (-1, 32))
    amax = np.abs(blocks).max(-1, keepdims=True)
    byte = np.maximum(np.where(amax > 0, np.frexp(amax)[1] - 1 + 127, 0) - down, 1)
    scale = np.exp2(byte - 127.0)
    codes = (blocks / scale).astype(np.float32).astype(dtype).astype(np.float64)
    return np.moveaxis((codes * scale).reshape(v.shape), -1, axis)


WIDE = False


def mx_kscale(k):
    if not WIDE:
        return np.ones(k)
    levels = np.array([10, -10, 5, -5, 0])
    if k % 512:
        return np.exp2(np.random.permutation(np.resize(levels, k // 32))).repeat(32)
    a = np.empty((k // 512, 16))
    for p in range(k // 512):
        a[p, :8] = np.random.permutation(np.resize(levels, 8))
        for g in range(8):
            far = levels[np.abs(levels - a[p, g]) >= 10]
            a[p, g + 8] = far[np.random.randint(len(far))]
    return np.exp2(a.ravel()).repeat(32)


def f64(x):
    return np.asarray(x).astype(np.float64)


def striped(idx):
    return np.tile(np.asarray(idx).reshape(-1, 16).T, (8, 1)).astype(np.uint16)


def unstriped(offs):
    return offs[:16].T.reshape(-1).astype(np.int64)


E2M1 = np.array([0.0, 0.5, 1.0, 1.5, 2.0, 3.0, 4.0, 6.0, -0.0, -0.5, -1.0, -1.5, -2.0, -3.0, -4.0, -6.0])


def pack_weight(w, fmt):
    k, n = w.shape
    w = f64(np.asarray(w, np.float32).astype(ml_dtypes.bfloat16)).reshape(k // 32, 32, n)
    amax = np.abs(w).max(1)
    if fmt == "e4m3":
        byte = np.frexp(amax)[1] - 1 + 127 - 7
    else:
        mant, ex = np.frexp(amax / 6.0)
        byte = np.where(mant > 0.5, ex, ex - 1) + 127
    byte = np.clip(np.where(amax > 0, byte, 1), 1, 254)
    scaled = (w * np.exp2(127.0 - byte)[:, None, :]).reshape(k, n).astype(np.float32)
    by_word = np.ascontiguousarray(scaled.reshape(k // 512, 128, 4, n).transpose(0, 1, 3, 2))
    if fmt == "e4m3":
        words = by_word.astype(ml_dtypes.float8_e4m3fn).view(np.uint8)
    else:
        c = by_word.astype(ml_dtypes.float4_e2m1fn).view(np.uint8) & 0xF
        words = (c[..., 0::2] | (c[..., 1::2] << 4)).reshape(k // 512, 128, 2 * n)
    return np.ascontiguousarray(words), np.ascontiguousarray(byte.astype(np.uint8).reshape(k // 512, 16, n))


def unpack_weight(words, scales, fmt):
    g, _, n = scales.shape
    words = np.ascontiguousarray(words).reshape(g, 128, n, -1)
    if fmt == "e4m3":
        vals = words.view(ml_dtypes.float8_e4m3fn).astype(np.float64)
    else:
        nib = np.empty((g, 128, n, 4), np.uint8)
        nib[..., 0::2] = words & 0xF
        nib[..., 1::2] = words >> 4
        vals = E2M1[nib]
    vals = vals * np.repeat(np.exp2(scales.astype(np.float64) - 127.0), 8, axis=1)[..., None]
    return vals.transpose(0, 1, 3, 2).reshape(g * 512, n)


D, T, I, J, U, Z, E, N = 512, 2048, 512, 512, 1024, 1024, 512, 64


def setup_inputs():
    n = np.random.standard_normal
    idx = np.random.permutation(T)[:I]
    idx2 = np.random.permutation(U)[:J]
    idx3 = np.random.permutation(Z)[:J]
    fd = mx_kscale(D)
    fi = mx_kscale(I)
    ti = np.ones(T)
    ti[idx] = fi
    keysp = pack_weight(n((D, T)) / fd[:, None], "e4m3")
    return {
        "keys_words": keysp[0],
        "keys_scales": keysp[1],
        "notes": (n((D, U)) * 1.0 / np.sqrt(D) * fd[:, None]).astype(np.float32),
        "users2": (n((D, Z)) * 1.0 / np.sqrt(D) * fd[:, None]).astype(np.float32),
        "rowf": (np.random.uniform(0.02, 0.08, (I, 1)) * fi[:, None]).astype(np.float32),
        "vals": (n((E, T)) / ti).astype(np.float32),
        "offs": striped(idx),
        "offs2": striped(idx2),
        "offs3": striped(idx3),
    }


def reference(keys_words, keys_scales, notes, users2, rowf, vals, offs, offs2, offs3):
    idx = unstriped(offs)
    idx2 = unstriped(offs2)
    idx3 = unstriped(offs3)
    keysu = unpack_weight(keys_words, keys_scales, "e4m3")
    keysidxg = keysu[:, idx]
    notesidx2q = mxq(f64(notes)[:, idx2], 0, "e4m3")
    g1 = keysidxg.T @ notesidx2q
    users2idx3q = mxq(f64(users2)[:, idx3], 0, "e4m3")
    g2 = keysidxg.T @ users2idx3q
    g0 = np.maximum(g1, g2)
    gr1 = g0 * f64(rowf)
    vt1 = f64(vals)[:, idx].T
    vt1q = mxq(vt1, 0, "e4m3")
    gr1q = mxq(gr1, 0, "e4m3")
    o = vt1q.T @ gr1q
    y = o.reshape(E, N, J // N).max(axis=2)
    return y

@@ -1,0 +1,204 @@
+from contextlib import ExitStack
+
+import concourse.mybir as mybir
+from concourse.masks import make_identity
+
+D, T, I, J, U, Z, E, N = 512, 2048, 512, 512, 1024, 1024, 512, 64
+FLOPS = 2 * D * I * J * 2 + 2 * I * E * J
+
+F32 = mybir.dt.float32
+BF16 = mybir.dt.bfloat16
+I32 = mybir.dt.int32
+U32 = mybir.dt.uint32
+U16 = mybir.dt.uint16
+U8 = mybir.dt.uint8
+FP8X4 = mybir.dt.float8_e4m3fn_x4
+MAX = mybir.AluOpType.max
+MULT = mybir.AluOpType.mult
+COPY = mybir.ActivationFunctionType.Copy
+AXIS_X = mybir.AxisListType.X
+
+P = 128
+PACK = 4
+HALF = J // 2
+CHUNK = 128
+CHUNKS = J // CHUNK
+RUN = J // N
+LIST_COLS = 32
+
+
+def tile_attend_tab_larger_bestruns_kernel(tc, keys_words, keys_scales, notes, users2, rowf, vals, offs, offs2, offs3, out):
+    nc = tc.nc
+    with ExitStack() as ctx:
+        sb = ctx.enter_context(tc.tile_pool(name="sb", bufs=1))
+        ps_g = ctx.enter_context(tc.psum_pool(name="ps_g", bufs=4))
+        ps_o = ctx.enter_context(tc.psum_pool(name="ps_o", bufs=4))
+
+        list_i = sb.tile([P, LIST_COLS], U16, name="list_i")
+        list_n = sb.tile([P, LIST_COLS], U16, name="list_n")
+        list_u = sb.tile([P, LIST_COLS], U16, name="list_u")
+        note_pl = [sb.tile([P, U], F32, name=f"note_pl{t}") for t in range(PACK)]
+        user_pl = [sb.tile([P, Z], F32, name=f"user_pl{t}", tag=f"user_pl{t}") for t in range(PACK)]
+        val_bl = [sb.tile([P, T], F32, name=f"val_bl{b}", tag=f"val_bl{b}", align_bytes=64) for b in range(E // P)]
+        key_words = sb.tile([P, T], U32, name="key_words")
+        key_scales = sb.tile([P, T], U8, name="key_scales")
+        factor = sb.tile([P, PACK], F32, name="factor")
+        ident = sb.tile([P, P], F32, name="ident")
+
+        notes_v = notes.rearrange("(p t) u -> t p u", t=PACK)
+        users_v = users2.rearrange("(p t) z -> t p z", t=PACK)
+
+        nc.vector.memset(key_scales[:].bitcast(I32), 0)
+        nc.sync.dma_start(note_pl[0][:], notes_v[0])
+        nc.sync.dma_start(list_n[:], offs2)
+        nc.sync.dma_start(list_i[:], offs)
+        nc.sync.dma_start(note_pl[1][:], notes_v[1])
+        nc.sync.dma_start(note_pl[2][:], notes_v[2])
+        for q in range(4):
+            nc.sync.dma_start(key_scales[32 * q : 32 * q + 4, :].bitcast(I32), keys_scales[0, 4 * q : 4 * q + 4, :].bitcast(I32))
+        nc.sync.dma_start(note_pl[3][:], notes_v[3])
+        nc.sync.dma_start(key_words[:].bitcast(I32), keys_words[0].rearrange("p n t -> p (n t)").bitcast(I32))
+        nc.sync.dma_start(list_u[:], offs3)
+        nc.sync.dma_start(factor[:], rowf.rearrange("(p r) o -> p (r o)", r=PACK))
+        for t in range(PACK):
+            nc.sync.dma_start(user_pl[t][:], users_v[t])
+        for b in range(E // P):
+            nc.sync.dma_start(val_bl[b][:], vals[b * P : (b + 1) * P, :])
+        make_identity(nc, ident[:])
+
+        def half_list(lst, h):
+            return lst[:, h * LIST_COLS // 2 : (h + 1) * LIST_COLS // 2]
+
+        def gather_planes(planes, lst, tags):
+            picked = [sb.tile([P, PACK, HALF], BF16, name=f"picked{h}", tag=tags[h], align_bytes=64) for h in range(2)]
+            for t in range(PACK):
+                nc.vector.tensor_copy(picked[0][:, t, :], planes[t][:].indirect(half_list(lst, 0)))
+                nc.scalar.activation(picked[1][:, t, :], planes[t][:].indirect(half_list(lst, 1)), COPY)
+            return picked
+
+        def quantize_planes(picked, tag):
+            woven = [sb.tile([P, HALF, PACK], BF16, name=f"{tag}_woven{h}", tag=f"{tag}_woven{h}", align_bytes=64) for h in range(2)]
+            codes = [sb.tile([P, HALF], U32, name=f"{tag}_codes{h}", align_bytes=64) for h in range(2)]
+            scales = [sb.tile([P, HALF], U8, name=f"{tag}_scales{h}", align_bytes=64) for h in range(2)]
+            for h in range(2):
+                nc.vector.tensor_copy(woven[h][:], picked[h][:].rearrange("p t j -> p j t"))
+            for h in range(2):
+                nc.vector.quantize_mx(out=codes[h][:].bitcast(FP8X4), scales=scales[h][:], in_=woven[h][:].rearrange("p j t -> p (j t)"))
+            return codes, scales
+
+        key_bytes = sb.tile([P, I], U8, name="key_bytes", align_bytes=64)
+
+        def table_chunk(codes, scales, c):
+            h, lo = divmod(c * CHUNK, HALF)
+            bank = ps_g.tile([P, PACK, CHUNK], F32, name="bank", tag="bank")
+            for r in range(PACK):
+                nc.tensor.matmul_mx(
+                    out=bank[:, r, :],
+                    lhsT=key_codes[:, r * P : (r + 1) * P].bitcast(FP8X4),
+                    lhsT_scale=key_bytes[:, r * P : (r + 1) * P],
+                    rhs=codes[h][:, lo : lo + CHUNK].bitcast(FP8X4),
+                    rhs_scale=scales[h][:, lo : lo + CHUNK],
+                    start=True,
+                    stop=True,
+                )
+            return bank
+
+        note_picked = gather_planes(note_pl, list_n, ("note_picked0", "note_picked1"))
+        nc.vector.tensor_copy(key_bytes[:].rearrange("p (r s) -> p s r", r=PACK), key_scales[:].indirect(list_i[:]))
+        note_codes, note_scales = quantize_planes(note_picked, "note")
+        key_codes = sb.tile([P, I], U32, name="key_codes", tag="note_picked1", align_bytes=64)
+        nc.vector.tensor_copy(key_codes[:].rearrange("p (r s) -> p s r", r=PACK), key_words[:].indirect(list_i[:]))
+        g1_banks = [table_chunk(note_codes, note_scales, c) for c in range(CHUNKS)]
+
+        user_picked = gather_planes(user_pl, list_u, ("note_woven1", "val_picked0"))
+        g1 = sb.tile([P, CHUNKS, CHUNK, PACK], F32, name="g1", tag=f"user_pl{PACK - 1}")
+        for c in range(CHUNKS):
+            nc.scalar.copy(g1[:, c], g1_banks[c][:].rearrange("p r j -> p j r"))
+        user_codes, user_scales = quantize_planes(user_picked, "user")
+        g2_banks = [table_chunk(user_codes, user_scales, c) for c in range(CHUNKS)]
+
+
+        def gather_values(b, tag):
+            picked = sb.tile([P, I], BF16, name="val_picked", tag=tag, align_bytes=64)
+            nc.scalar.activation(picked[:], val_bl[b][:].indirect(list_i[:]), COPY)
+            return picked
+
+        def gather_values_shared(b, tag):
+            picked = sb.tile([P, I], BF16, name="val_picked", tag=tag, align_bytes=64)
+            nc.vector.tensor_copy(picked[:, :HALF], val_bl[b][:].indirect(half_list(list_i, 0)))
+            nc.scalar.activation(picked[:, HALF:], val_bl[b][:].indirect(half_list(list_i, 1)), COPY)
+            return picked
+
+        def turn_values(b, picked):
+            words = picked[:].bitcast(F32)
+            turned = ps_g.tile([P, 2, P], F32, name="turned", tag="bank")
+            for u in range(2):
+                nc.tensor.transpose(turned[:, u, :], words[:, u::2], ident[:])
+            nc.scalar.copy(vt_woven[b].bitcast(F32), turned[:].rearrange("p u e -> p e u"))
+
+        def quantize_values(woven, width, tag):
+            codes = sb.tile([P, width], U32, name="vt_codes", tag=tag, align_bytes=64)
+            scales = sb.tile([P, width], U8, name="vt_scales", tag=tag + "_scales", align_bytes=64)
+            nc.vector.quantize_mx(out=codes[:].bitcast(FP8X4), scales=scales[:], in_=woven)
+            return codes, scales
+
+        larger = [sb.tile([P, CHUNK, PACK], F32, name=f"larger{c}", tag=f"larger{c}", align_bytes=64) for c in range(CHUNKS)]
+        gr_woven = [sb.tile([P, CHUNK, PACK], BF16, name=f"gr_woven{c}", tag=f"gr_woven{c}", align_bytes=64) for c in range(CHUNKS)]
+        gr_codes = sb.tile([P, J], U32, name="gr_codes", align_bytes=64)
+        gr_scales = sb.tile([P, J], U8, name="gr_scales", align_bytes=64)
+
+        def take_larger(c):
+            nc.vector.tensor_tensor(larger[c][:], g2_banks[c][:].rearrange("p r j -> p j r"), g1[:, c], MAX)
+
+        def apply_factor(c):
+            nc.vector.tensor_tensor(gr_woven[c][:], larger[c][:], factor[:].unsqueeze(1).to_broadcast([P, CHUNK, PACK]), MULT)
+
+        def quantize_table(c):
+            cols = slice(c * CHUNK, (c + 1) * CHUNK)
+            nc.vector.quantize_mx(out=gr_codes[:, cols].bitcast(FP8X4), scales=gr_scales[:, cols], in_=gr_woven[c][:].rearrange("p j r -> p (j r)"))
+
+        def finish_block(b, codes, scales, parts):
+            width = J // parts
+            for part in range(parts):
+                cols = slice(part * width, (part + 1) * width)
+                sums = ps_o.tile([P, width], F32, name="sums", tag="sums")
+                nc.tensor.matmul_mx(
+                    out=sums[:],
+                    lhsT=codes.bitcast(FP8X4),
+                    lhsT_scale=scales,
+                    rhs=gr_codes[:, cols].bitcast(FP8X4),
+                    rhs_scale=gr_scales[:, cols],
+                    start=True,
+                    stop=True,
+                )
+                runs = slice(part * width // RUN, (part + 1) * width // RUN)
+                nc.vector.tensor_reduce(best[:, b, runs], sums[:].rearrange("p (n k) -> p n k", k=RUN), AXIS_X, MAX)
+
+        picked = [gather_values(0, "val_picked0"), gather_values(1, "note_woven1")]
+        first_woven = sb.tile([P, 2, P, PACK], BF16, name="first_woven", tag="val_bl1", align_bytes=64)
+        later_woven = [sb.tile([P, P, PACK], BF16, name=f"later_woven{b}", align_bytes=64) for b in range(2)]
+        vt_woven = [first_woven[:, 0], first_woven[:, 1], later_woven[0][:], later_woven[1][:]]
+        for step in range(CHUNKS + 2):
+            if step < CHUNKS:
+                take_larger(step)
+            if step < 2:
+                turn_values(step, picked[step])
+            if step == 2:
+                turn_values(2, gather_values(2, "note_woven1"))
+            if 1 <= step <= CHUNKS:
+                apply_factor(step - 1)
+            if step >= 2:
+                quantize_table(step - 2)
+        first_codes, first_scales = quantize_values(first_woven[:].rearrange("p b e t -> p (b e t)"), 2 * P, "note_woven1")
+        codes, scales = quantize_values(later_woven[0][:].rearrange("p e t -> p (e t)"), P, "gr_woven2")
+        last_picked = gather_values_shared(3, "gr_woven3")
+        best = sb.tile([P, E // P, N], F32, name="best", tag="val_bl3", align_bytes=64)
+        out_v = out.rearrange("(b p) n -> p b n", p=P)
+        finish_block(0, first_codes[:, :P], first_scales[:, :P], 1)
+        finish_block(1, first_codes[:, P:], first_scales[:, P:], 1)
+        turn_values(3, last_picked)
+        last_codes, last_scales = quantize_values(later_woven[1][:].rearrange("p e t -> p (e t)"), P, "last_codes")
+        finish_block(2, codes[:], scales[:], 1)
+        nc.sync.dma_start(out_v[:, :3, :], best[:, :3, :])
+        finish_block(3, last_codes[:], last_scales[:], 2)
+        nc.sync.dma_start(out_v[:, 3, :], best[:, 3, :])

@@ -31,65 +31,85 @@ def tile_attend_tab_larger_bestruns_kernel(tc, keys_words, keys_scales, notes, u
     nc = tc.nc
     with ExitStack() as ctx:
         sb = ctx.enter_context(tc.tile_pool(name="sb", bufs=1))
+        tail = ctx.enter_context(tc.tile_pool(name="tail", bufs=1))
         ps_g = ctx.enter_context(tc.psum_pool(name="ps_g", bufs=4))
-        ps_o = ctx.enter_context(tc.psum_pool(name="ps_o", bufs=4))
+        ps_o = ctx.enter_context(tc.psum_pool(name="ps_o", bufs=3))
+        ps_f = ctx.enter_context(tc.psum_pool(name="ps_f", bufs=1))
 
         list_i = sb.tile([P, LIST_COLS], U16, name="list_i")
         list_n = sb.tile([P, LIST_COLS], U16, name="list_n")
         list_u = sb.tile([P, LIST_COLS], U16, name="list_u")
         note_pl = [sb.tile([P, U], F32, name=f"note_pl{t}") for t in range(PACK)]
         user_pl = [sb.tile([P, Z], F32, name=f"user_pl{t}", tag=f"user_pl{t}") for t in range(PACK)]
-        val_bl = [sb.tile([P, T], F32, name=f"val_bl{b}", tag=f"val_bl{b}", align_bytes=64) for b in range(E // P)]
+        val_bl = [sb.tile([P, T], F32, name=f"val_bl{b}", tag=f"val_bl{b}", align_bytes=64) for b in range(3)]
+        val_bl.append(tail.tile([P, T], F32, name="val_bl3", align_bytes=64, offset=0))
         key_words = sb.tile([P, T], U32, name="key_words")
         key_scales = sb.tile([P, T], U8, name="key_scales")
-        factor = sb.tile([P, PACK], F32, name="factor")
+        factor = sb.tile([P, P], F32, name="factor")
         ident = sb.tile([P, P], F32, name="ident")
 
         notes_v = notes.rearrange("(p t) u -> t p u", t=PACK)
         users_v = users2.rearrange("(p t) z -> t p z", t=PACK)
 
         nc.vector.memset(key_scales[:].bitcast(I32), 0)
+        nc.gpsimd.memset(factor[:], 0.0)
         nc.sync.dma_start(note_pl[0][:], notes_v[0])
         nc.sync.dma_start(list_n[:], offs2)
+        for t in range(1, PACK):
+            nc.sync.dma_start(note_pl[t][:], notes_v[t])
         nc.sync.dma_start(list_i[:], offs)
-        nc.sync.dma_start(note_pl[1][:], notes_v[1])
-        nc.sync.dma_start(note_pl[2][:], notes_v[2])
         for q in range(4):
             nc.sync.dma_start(key_scales[32 * q : 32 * q + 4, :].bitcast(I32), keys_scales[0, 4 * q : 4 * q + 4, :].bitcast(I32))
-        nc.sync.dma_start(note_pl[3][:], notes_v[3])
         nc.sync.dma_start(key_words[:].bitcast(I32), keys_words[0].rearrange("p n t -> p (n t)").bitcast(I32))
         nc.sync.dma_start(list_u[:], offs3)
-        nc.sync.dma_start(factor[:], rowf.rearrange("(p r) o -> p (r o)", r=PACK))
+        nc.sync.dma_start(factor[:, :PACK], rowf.rearrange("(p r) o -> p (r o)", r=PACK))
         for t in range(PACK):
             nc.sync.dma_start(user_pl[t][:], users_v[t])
         for b in range(E // P):
             nc.sync.dma_start(val_bl[b][:], vals[b * P : (b + 1) * P, :])
         make_identity(nc, ident[:])
 
+        factor_rows_ps = ps_o.tile([P, P], F32, name="factor_rows_ps", tag="sums")
+        nc.tensor.transpose(factor_rows_ps[:], factor[:], ident[:])
+        factor_rows = sb.tile([P, P], F32, name="factor_rows")
+        nc.scalar.copy(factor_rows[:], factor_rows_ps[:])
+        factor_ps = ps_f.tile([P, P], F32, name="factor_ps")
+        nc.tensor.transpose(factor_ps[:], factor_rows[:], ident[:])
+
         def half_list(lst, h):
             return lst[:, h * LIST_COLS // 2 : (h + 1) * LIST_COLS // 2]
 
-        def gather_planes(planes, lst, tags):
-            picked = [sb.tile([P, PACK, HALF], BF16, name=f"picked{h}", tag=tags[h], align_bytes=64) for h in range(2)]
+        def gather_planes(planes, lst, tag, shared):
+            picked = sb.tile([P, PACK, J], BF16, name="picked", tag=tag, align_bytes=64)
             for t in range(PACK):
-                nc.vector.tensor_copy(picked[0][:, t, :], planes[t][:].indirect(half_list(lst, 0)))
-                nc.scalar.activation(picked[1][:, t, :], planes[t][:].indirect(half_list(lst, 1)), COPY)
+                if t in shared:
+                    nc.vector.tensor_copy(picked[:, t, :HALF], planes[t][:].indirect(half_list(lst, 0)))
+                    nc.scalar.activation(picked[:, t, HALF:], planes[t][:].indirect(half_list(lst, 1)), COPY)
+                else:
+                    nc.scalar.activation(picked[:, t, :], planes[t][:].indirect(lst[:]), COPY)
             return picked
 
-        def quantize_planes(picked, tag):
-            woven = [sb.tile([P, HALF, PACK], BF16, name=f"{tag}_woven{h}", tag=f"{tag}_woven{h}", align_bytes=64) for h in range(2)]
-            codes = [sb.tile([P, HALF], U32, name=f"{tag}_codes{h}", align_bytes=64) for h in range(2)]
-            scales = [sb.tile([P, HALF], U8, name=f"{tag}_scales{h}", align_bytes=64) for h in range(2)]
-            for h in range(2):
-                nc.vector.tensor_copy(woven[h][:], picked[h][:].rearrange("p t j -> p j t"))
-            for h in range(2):
-                nc.vector.quantize_mx(out=codes[h][:].bitcast(FP8X4), scales=scales[h][:], in_=woven[h][:].rearrange("p j t -> p (j t)"))
+        def quantize_planes(picked, tag, pieces, on_scalar):
+            width = J // pieces
+            woven = [sb.tile([P, width, PACK], BF16, name=f"{tag}_woven{h}", tag=f"{tag}_woven{h}", align_bytes=64) for h in range(pieces)]
+            codes = [sb.tile([P, width], U32, name=f"{tag}_codes{h}", align_bytes=64) for h in range(pieces)]
+            scales = [sb.tile([P, width], U8, name=f"{tag}_scales{h}", align_bytes=64) for h in range(pieces)]
+            for step in range(pieces + 1):
+                if step < pieces:
+                    weave = nc.scalar.copy if step in on_scalar else nc.vector.tensor_copy
+                    weave(
+                        woven[step][:].rearrange("p (c i) t -> p c t i", i=4),
+                        picked[:, :, step * width : (step + 1) * width].rearrange("p t (c i) -> p c t i", i=4),
+                    )
+                if step >= 1:
+                    h = step - 1
+                    nc.vector.quantize_mx(out=codes[h][:].bitcast(FP8X4), scales=scales[h][:], in_=woven[h][:].rearrange("p j t -> p (j t)"))
             return codes, scales
 
         key_bytes = sb.tile([P, I], U8, name="key_bytes", align_bytes=64)
 
         def table_chunk(codes, scales, c):
-            h, lo = divmod(c * CHUNK, HALF)
+            h, lo = divmod(c * CHUNK, J // len(codes))
             bank = ps_g.tile([P, PACK, CHUNK], F32, name="bank", tag="bank")
             for r in range(PACK):
                 nc.tensor.matmul_mx(
@@ -103,18 +123,21 @@ def tile_attend_tab_larger_bestruns_kernel(tc, keys_words, keys_scales, notes, u
                 )
             return bank
 
-        note_picked = gather_planes(note_pl, list_n, ("note_picked0", "note_picked1"))
+        note_picked = gather_planes(note_pl, list_n, "note_picked", (0, 1, 2, 3))
         nc.vector.tensor_copy(key_bytes[:].rearrange("p (r s) -> p s r", r=PACK), key_scales[:].indirect(list_i[:]))
-        note_codes, note_scales = quantize_planes(note_picked, "note")
-        key_codes = sb.tile([P, I], U32, name="key_codes", tag="note_picked1", align_bytes=64)
+        note_codes, note_scales = quantize_planes(note_picked, "note", 2, ())
+        key_codes = sb.tile([P, I], U32, name="key_codes", tag="note_picked", align_bytes=64)
         nc.vector.tensor_copy(key_codes[:].rearrange("p (r s) -> p s r", r=PACK), key_words[:].indirect(list_i[:]))
         g1_banks = [table_chunk(note_codes, note_scales, c) for c in range(CHUNKS)]
 
-        user_picked = gather_planes(user_pl, list_u, ("note_woven1", "val_picked0"))
-        g1 = sb.tile([P, CHUNKS, CHUNK, PACK], F32, name="g1", tag=f"user_pl{PACK - 1}")
-        for c in range(CHUNKS):
-            nc.scalar.copy(g1[:, c], g1_banks[c][:].rearrange("p r j -> p j r"))
-        user_codes, user_scales = quantize_planes(user_picked, "user")
+        user_picked = gather_planes(user_pl, list_u, "note_woven1", (1, 2, 3))
+        g1_first = sb.tile([P, CHUNK, PACK], F32, name="g1_first", tag="user_pl2")
+        g1_rest = sb.tile([P, CHUNKS - 1, CHUNK, PACK], F32, name="g1_rest", tag="user_pl3")
+        g1 = [g1_first[:]] + [g1_rest[:, c] for c in range(CHUNKS - 1)]
+        nc.scalar.copy(g1[0], g1_banks[0][:].rearrange("p r j -> p j r"))
+        user_codes, user_scales = quantize_planes(user_picked, "user", CHUNKS, (CHUNKS - 1,))
+        for c in range(1, CHUNKS):
+            nc.scalar.copy(g1[c], g1_banks[c][:].rearrange("p r j -> p j r"))
         g2_banks = [table_chunk(user_codes, user_scales, c) for c in range(CHUNKS)]
 
 
@@ -136,26 +159,22 @@ def tile_attend_tab_larger_bestruns_kernel(tc, keys_words, keys_scales, notes, u
                 nc.tensor.transpose(turned[:, u, :], words[:, u::2], ident[:])
             nc.scalar.copy(vt_woven[b].bitcast(F32), turned[:].rearrange("p u e -> p e u"))
 
-        def quantize_values(woven, width, tag):
-            codes = sb.tile([P, width], U32, name="vt_codes", tag=tag, align_bytes=64)
-            scales = sb.tile([P, width], U8, name="vt_scales", tag=tag + "_scales", align_bytes=64)
+        def quantize_values(woven, codes, name):
+            scales = sb.tile(list(codes.shape), U8, name=name, align_bytes=64)
             nc.vector.quantize_mx(out=codes[:].bitcast(FP8X4), scales=scales[:], in_=woven)
             return codes, scales
 
-        larger = [sb.tile([P, CHUNK, PACK], F32, name=f"larger{c}", tag=f"larger{c}", align_bytes=64) for c in range(CHUNKS)]
-        gr_woven = [sb.tile([P, CHUNK, PACK], BF16, name=f"gr_woven{c}", tag=f"gr_woven{c}", align_bytes=64) for c in range(CHUNKS)]
+        larger = [sb.tile([P, 2, CHUNK, PACK], F32, name=f"larger{h}") for h in range(2)]
+        gr_woven = [sb.tile([P, 2, CHUNK, PACK], BF16, name=f"gr_woven{h}", tag=f"gr_woven{h}", align_bytes=64) for h in range(2)]
         gr_codes = sb.tile([P, J], U32, name="gr_codes", align_bytes=64)
         gr_scales = sb.tile([P, J], U8, name="gr_scales", align_bytes=64)
 
         def take_larger(c):
-            nc.vector.tensor_tensor(larger[c][:], g2_banks[c][:].rearrange("p r j -> p j r"), g1[:, c], MAX)
+            nc.vector.tensor_tensor(larger[c // 2][:, c % 2], g2_banks[c][:].rearrange("p r j -> p j r"), g1[c], MAX)
 
-        def apply_factor(c):
-            nc.vector.tensor_tensor(gr_woven[c][:], larger[c][:], factor[:].unsqueeze(1).to_broadcast([P, CHUNK, PACK]), MULT)
-
-        def quantize_table(c):
-            cols = slice(c * CHUNK, (c + 1) * CHUNK)
-            nc.vector.quantize_mx(out=gr_codes[:, cols].bitcast(FP8X4), scales=gr_scales[:, cols], in_=gr_woven[c][:].rearrange("p j r -> p (j r)"))
+        def quantize_table(h):
+            cols = slice(h * HALF, (h + 1) * HALF)
+            nc.vector.quantize_mx(out=gr_codes[:, cols].bitcast(FP8X4), scales=gr_scales[:, cols], in_=gr_woven[h][:].rearrange("p c j r -> p (c j r)"))
 
         def finish_block(b, codes, scales, parts):
             width = J // parts
@@ -174,30 +193,37 @@ def tile_attend_tab_larger_bestruns_kernel(tc, keys_words, keys_scales, notes, u
                 runs = slice(part * width // RUN, (part + 1) * width // RUN)
                 nc.vector.tensor_reduce(best[:, b, runs], sums[:].rearrange("p (n k) -> p n k", k=RUN), AXIS_X, MAX)
 
-        picked = [gather_values(0, "val_picked0"), gather_values(1, "note_woven1")]
+        picked = [gather_values(0, "note_woven1"), gather_values(1, "val_picked1")]
         first_woven = sb.tile([P, 2, P, PACK], BF16, name="first_woven", tag="val_bl1", align_bytes=64)
         later_woven = [sb.tile([P, P, PACK], BF16, name=f"later_woven{b}", align_bytes=64) for b in range(2)]
         vt_woven = [first_woven[:, 0], first_woven[:, 1], later_woven[0][:], later_woven[1][:]]
-        for step in range(CHUNKS + 2):
-            if step < CHUNKS:
-                take_larger(step)
-            if step < 2:
-                turn_values(step, picked[step])
-            if step == 2:
-                turn_values(2, gather_values(2, "note_woven1"))
-            if 1 <= step <= CHUNKS:
-                apply_factor(step - 1)
-            if step >= 2:
-                quantize_table(step - 2)
-        first_codes, first_scales = quantize_values(first_woven[:].rearrange("p b e t -> p (b e t)"), 2 * P, "note_woven1")
-        codes, scales = quantize_values(later_woven[0][:].rearrange("p e t -> p (e t)"), P, "gr_woven2")
-        last_picked = gather_values_shared(3, "gr_woven3")
-        best = sb.tile([P, E // P, N], F32, name="best", tag="val_bl3", align_bytes=64)
+        for c in range(CHUNKS):
+            take_larger(c)
+        for c in range(2):
+            nc.gpsimd.tensor_tensor(gr_woven[0][:, c], larger[0][:, c], factor[:, :PACK].unsqueeze(1).to_broadcast([P, CHUNK, PACK]), MULT)
+        nc.vector.tensor_tensor(
+            gr_woven[1][:].rearrange("p c j r -> p (c j) r"),
+            larger[1][:].rearrange("p c j r -> p (c j) r"),
+            factor_ps[:, :PACK].unsqueeze(1).to_broadcast([P, HALF, PACK]),
+            MULT,
+        )
+        for h in range(2):
+            quantize_table(h)
+        turn_values(0, picked[0])
+        turn_values(1, picked[1])
+        turn_values(2, gather_values(2, "val_picked1"))
+        first_codes = sb.tile([P, 2 * P], U32, name="first_codes", tag="val_picked1", align_bytes=64)
+        first_codes, first_scales = quantize_values(first_woven[:].rearrange("p b e t -> p (b e t)"), first_codes, "first_scales")
+        last_picked = gather_values_shared(3, "gr_woven1")
+        codes = tail.tile([P, P], U32, name="third_codes", align_bytes=64, offset=0)
+        codes, scales = quantize_values(later_woven[0][:].rearrange("p e t -> p (e t)"), codes, "third_scales")
+        best = tail.tile([P, E // P, N], F32, name="best", align_bytes=64, offset=1024)
         out_v = out.rearrange("(b p) n -> p b n", p=P)
+        turn_values(3, last_picked)
         finish_block(0, first_codes[:, :P], first_scales[:, :P], 1)
         finish_block(1, first_codes[:, P:], first_scales[:, P:], 1)
-        turn_values(3, last_picked)
-        last_codes, last_scales = quantize_values(later_woven[1][:].rearrange("p e t -> p (e t)"), P, "last_codes")
+        last_codes = sb.tile([P, P], U32, name="last_codes", align_bytes=64)
+        last_codes, last_scales = quantize_values(later_woven[1][:].rearrange("p e t -> p (e t)"), last_codes, "last_scales")
         finish_block(2, codes[:], scales[:], 1)
         nc.sync.dma_start(out_v[:, :3, :], best[:, :3, :])
         finish_block(3, last_codes[:], last_scales[:], 2)

@@ -51,10 +51,11 @@ def tile_attend_tab_larger_bestruns_kernel(tc, keys_words, keys_scales, notes, u
         notes_v = notes.rearrange("(p t) u -> t p u", t=PACK)
         users_v = users2.rearrange("(p t) z -> t p z", t=PACK)
 
+        nc.vector.memset(factor[:], 0.0)
         nc.vector.memset(key_scales[:].bitcast(I32), 0)
-        nc.gpsimd.memset(factor[:], 0.0)
         nc.sync.dma_start(note_pl[0][:], notes_v[0])
         nc.sync.dma_start(list_n[:], offs2)
+        nc.sync.dma_start(factor[:, :PACK], rowf.rearrange("(p r) o -> p (r o)", r=PACK))
         for t in range(1, PACK):
             nc.sync.dma_start(note_pl[t][:], notes_v[t])
         nc.sync.dma_start(list_i[:], offs)
@@ -62,7 +63,6 @@ def tile_attend_tab_larger_bestruns_kernel(tc, keys_words, keys_scales, notes, u
             nc.sync.dma_start(key_scales[32 * q : 32 * q + 4, :].bitcast(I32), keys_scales[0, 4 * q : 4 * q + 4, :].bitcast(I32))
         nc.sync.dma_start(key_words[:].bitcast(I32), keys_words[0].rearrange("p n t -> p (n t)").bitcast(I32))
         nc.sync.dma_start(list_u[:], offs3)
-        nc.sync.dma_start(factor[:, :PACK], rowf.rearrange("(p r) o -> p (r o)", r=PACK))
         for t in range(PACK):
             nc.sync.dma_start(user_pl[t][:], users_v[t])
         for b in range(E // P):
@@ -89,15 +89,14 @@ def tile_attend_tab_larger_bestruns_kernel(tc, keys_words, keys_scales, notes, u
                     nc.scalar.activation(picked[:, t, :], planes[t][:].indirect(lst[:]), COPY)
             return picked
 
-        def quantize_planes(picked, tag, pieces, on_scalar):
+        def quantize_planes(picked, tag, pieces):
             width = J // pieces
             woven = [sb.tile([P, width, PACK], BF16, name=f"{tag}_woven{h}", tag=f"{tag}_woven{h}", align_bytes=64) for h in range(pieces)]
             codes = [sb.tile([P, width], U32, name=f"{tag}_codes{h}", align_bytes=64) for h in range(pieces)]
             scales = [sb.tile([P, width], U8, name=f"{tag}_scales{h}", align_bytes=64) for h in range(pieces)]
             for step in range(pieces + 1):
                 if step < pieces:
-                    weave = nc.scalar.copy if step in on_scalar else nc.vector.tensor_copy
-                    weave(
+                    nc.vector.tensor_copy(
                         woven[step][:].rearrange("p (c i) t -> p c t i", i=4),
                         picked[:, :, step * width : (step + 1) * width].rearrange("p t (c i) -> p c t i", i=4),
                     )
@@ -125,7 +124,7 @@ def tile_attend_tab_larger_bestruns_kernel(tc, keys_words, keys_scales, notes, u
 
         note_picked = gather_planes(note_pl, list_n, "note_picked", (0, 1, 2, 3))
         nc.vector.tensor_copy(key_bytes[:].rearrange("p (r s) -> p s r", r=PACK), key_scales[:].indirect(list_i[:]))
-        note_codes, note_scales = quantize_planes(note_picked, "note", 2, ())
+        note_codes, note_scales = quantize_planes(note_picked, "note", 2)
         key_codes = sb.tile([P, I], U32, name="key_codes", tag="note_picked", align_bytes=64)
         nc.vector.tensor_copy(key_codes[:].rearrange("p (r s) -> p s r", r=PACK), key_words[:].indirect(list_i[:]))
         g1_banks = [table_chunk(note_codes, note_scales, c) for c in range(CHUNKS)]
@@ -135,7 +134,7 @@ def tile_attend_tab_larger_bestruns_kernel(tc, keys_words, keys_scales, notes, u
         g1_rest = sb.tile([P, CHUNKS - 1, CHUNK, PACK], F32, name="g1_rest", tag="user_pl3")
         g1 = [g1_first[:]] + [g1_rest[:, c] for c in range(CHUNKS - 1)]
         nc.scalar.copy(g1[0], g1_banks[0][:].rearrange("p r j -> p j r"))
-        user_codes, user_scales = quantize_planes(user_picked, "user", CHUNKS, (CHUNKS - 1,))
+        user_codes, user_scales = quantize_planes(user_picked, "user", CHUNKS)
         for c in range(1, CHUNKS):
             nc.scalar.copy(g1[c], g1_banks[c][:].rearrange("p r j -> p j r"))
         g2_banks = [table_chunk(user_codes, user_scales, c) for c in range(CHUNKS)]
@@ -160,9 +159,9 @@ def tile_attend_tab_larger_bestruns_kernel(tc, keys_words, keys_scales, notes, u
             nc.scalar.copy(vt_woven[b].bitcast(F32), turned[:].rearrange("p u e -> p e u"))
 
         def quantize_values(woven, codes, name):
-            scales = sb.tile(list(codes.shape), U8, name=name, align_bytes=64)
-            nc.vector.quantize_mx(out=codes[:].bitcast(FP8X4), scales=scales[:], in_=woven)
-            return codes, scales
+            scales = sb.tile([P, P], U8, name=name, align_bytes=64)
+            nc.vector.quantize_mx(out=codes.bitcast(FP8X4), scales=scales[:], in_=woven.rearrange("p e t -> p (e t)"))
+            return scales
 
         larger = [sb.tile([P, 2, CHUNK, PACK], F32, name=f"larger{h}") for h in range(2)]
         gr_woven = [sb.tile([P, 2, CHUNK, PACK], BF16, name=f"gr_woven{h}", tag=f"gr_woven{h}", align_bytes=64) for h in range(2)]
@@ -194,9 +193,10 @@ def tile_attend_tab_larger_bestruns_kernel(tc, keys_words, keys_scales, notes, u
                 nc.vector.tensor_reduce(best[:, b, runs], sums[:].rearrange("p (n k) -> p n k", k=RUN), AXIS_X, MAX)
 
         picked = [gather_values(0, "note_woven1"), gather_values(1, "val_picked1")]
-        first_woven = sb.tile([P, 2, P, PACK], BF16, name="first_woven", tag="val_bl1", align_bytes=64)
+        third_picked = gather_values(2, "val_picked2")
+        first_woven = [sb.tile([P, P, PACK], BF16, name="first_woven", tag=f"val_bl{b + 1}", align_bytes=64) for b in range(2)]
         later_woven = [sb.tile([P, P, PACK], BF16, name=f"later_woven{b}", align_bytes=64) for b in range(2)]
-        vt_woven = [first_woven[:, 0], first_woven[:, 1], later_woven[0][:], later_woven[1][:]]
+        vt_woven = [first_woven[0][:], first_woven[1][:], later_woven[0][:], later_woven[1][:]]
         for c in range(CHUNKS):
             take_larger(c)
         for c in range(2):
@@ -211,19 +211,19 @@ def tile_attend_tab_larger_bestruns_kernel(tc, keys_words, keys_scales, notes, u
             quantize_table(h)
         turn_values(0, picked[0])
         turn_values(1, picked[1])
-        turn_values(2, gather_values(2, "val_picked1"))
-        first_codes = sb.tile([P, 2 * P], U32, name="first_codes", tag="val_picked1", align_bytes=64)
-        first_codes, first_scales = quantize_values(first_woven[:].rearrange("p b e t -> p (b e t)"), first_codes, "first_scales")
+        turn_values(2, third_picked)
+        first_codes = sb.tile([P, 2, P], U32, name="first_codes", tag="val_picked2", align_bytes=64)
+        first_scales = [quantize_values(vt_woven[b], first_codes[:, b], f"first_scales{b}") for b in range(2)]
         last_picked = gather_values_shared(3, "gr_woven1")
         codes = tail.tile([P, P], U32, name="third_codes", align_bytes=64, offset=0)
-        codes, scales = quantize_values(later_woven[0][:].rearrange("p e t -> p (e t)"), codes, "third_scales")
+        scales = quantize_values(vt_woven[2], codes[:], "third_scales")
         best = tail.tile([P, E // P, N], F32, name="best", align_bytes=64, offset=1024)
         out_v = out.rearrange("(b p) n -> p b n", p=P)
         turn_values(3, last_picked)
-        finish_block(0, first_codes[:, :P], first_scales[:, :P], 1)
-        finish_block(1, first_codes[:, P:], first_scales[:, P:], 1)
+        finish_block(0, first_codes[:, 0], first_scales[0][:], 1)
+        finish_block(1, first_codes[:, 1], first_scales[1][:], 1)
         last_codes = sb.tile([P, P], U32, name="last_codes", align_bytes=64)
-        last_codes, last_scales = quantize_values(later_woven[1][:].rearrange("p e t -> p (e t)"), last_codes, "last_scales")
+        last_scales = quantize_values(vt_woven[3], last_codes[:], "last_scales")
         finish_block(2, codes[:], scales[:], 1)
         nc.sync.dma_start(out_v[:, :3, :], best[:, :3, :])
         finish_block(3, last_codes[:], last_scales[:], 2)

from contextlib import ExitStack

import concourse.mybir as mybir
from concourse.masks import make_identity

D, T, I, J, U, Z, E, N = 512, 2048, 512, 512, 1024, 1024, 512, 64
FLOPS = 2 * D * I * J * 2 + 2 * I * E * J

F32 = mybir.dt.float32
BF16 = mybir.dt.bfloat16
I32 = mybir.dt.int32
U32 = mybir.dt.uint32
U16 = mybir.dt.uint16
U8 = mybir.dt.uint8
FP8X4 = mybir.dt.float8_e4m3fn_x4
MAX = mybir.AluOpType.max
MULT = mybir.AluOpType.mult
COPY = mybir.ActivationFunctionType.Copy
AXIS_X = mybir.AxisListType.X

P = 128
PACK = 4
HALF = J // 2
CHUNK = 128
CHUNKS = J // CHUNK
RUN = J // N
LIST_COLS = 32


def tile_attend_tab_larger_bestruns_kernel(tc, keys_words, keys_scales, notes, users2, rowf, vals, offs, offs2, offs3, out):
    nc = tc.nc
    with ExitStack() as ctx:
        sb = ctx.enter_context(tc.tile_pool(name="sb", bufs=1))
        tail = ctx.enter_context(tc.tile_pool(name="tail", bufs=1))
        ps_g = ctx.enter_context(tc.psum_pool(name="ps_g", bufs=4))
        ps_o = ctx.enter_context(tc.psum_pool(name="ps_o", bufs=3))
        ps_f = ctx.enter_context(tc.psum_pool(name="ps_f", bufs=1))

        list_i = sb.tile([P, LIST_COLS], U16, name="list_i")
        list_n = sb.tile([P, LIST_COLS], U16, name="list_n")
        list_u = sb.tile([P, LIST_COLS], U16, name="list_u")
        note_pl = [sb.tile([P, U], F32, name=f"note_pl{t}") for t in range(PACK)]
        user_pl = [sb.tile([P, Z], F32, name=f"user_pl{t}", tag=f"user_pl{t}") for t in range(PACK)]
        val_bl = [sb.tile([P, T], F32, name=f"val_bl{b}", tag=f"val_bl{b}", align_bytes=64) for b in range(3)]
        val_bl.append(tail.tile([P, T], F32, name="val_bl3", align_bytes=64, offset=0))
        key_words = sb.tile([P, T], U32, name="key_words")
        key_scales = sb.tile([P, T], U8, name="key_scales")
        factor = sb.tile([P, P], F32, name="factor")
        ident = sb.tile([P, P], F32, name="ident")

        notes_v = notes.rearrange("(p t) u -> t p u", t=PACK)
        users_v = users2.rearrange("(p t) z -> t p z", t=PACK)

        nc.vector.memset(factor[:], 0.0)
        nc.vector.memset(key_scales[:].bitcast(I32), 0)
        nc.sync.dma_start(note_pl[0][:], notes_v[0])
        nc.sync.dma_start(list_n[:], offs2)
        nc.sync.dma_start(factor[:, :PACK], rowf.rearrange("(p r) o -> p (r o)", r=PACK))
        for t in range(1, PACK):
            nc.sync.dma_start(note_pl[t][:], notes_v[t])
        nc.sync.dma_start(list_i[:], offs)
        for q in range(4):
            nc.sync.dma_start(key_scales[32 * q : 32 * q + 4, :].bitcast(I32), keys_scales[0, 4 * q : 4 * q + 4, :].bitcast(I32))
        nc.sync.dma_start(key_words[:].bitcast(I32), keys_words[0].rearrange("p n t -> p (n t)").bitcast(I32))
        nc.sync.dma_start(list_u[:], offs3)
        for t in range(PACK):
            nc.sync.dma_start(user_pl[t][:], users_v[t])
        for b in range(E // P):
            nc.sync.dma_start(val_bl[b][:], vals[b * P : (b + 1) * P, :])
        make_identity(nc, ident[:])

        factor_rows_ps = ps_o.tile([P, P], F32, name="factor_rows_ps", tag="sums")
        nc.tensor.transpose(factor_rows_ps[:], factor[:], ident[:])
        factor_rows = sb.tile([P, P], F32, name="factor_rows")
        nc.scalar.copy(factor_rows[:], factor_rows_ps[:])
        factor_ps = ps_f.tile([P, P], F32, name="factor_ps")
        nc.tensor.transpose(factor_ps[:], factor_rows[:], ident[:])

        def half_list(lst, h):
            return lst[:, h * LIST_COLS // 2 : (h + 1) * LIST_COLS // 2]

        def gather_planes(planes, lst, tag, shared):
            picked = sb.tile([P, PACK, J], BF16, name="picked", tag=tag, align_bytes=64)
            for t in range(PACK):
                if t in shared:
                    nc.vector.tensor_copy(picked[:, t, :HALF], planes[t][:].indirect(half_list(lst, 0)))
                    nc.scalar.activation(picked[:, t, HALF:], planes[t][:].indirect(half_list(lst, 1)), COPY)
                else:
                    nc.scalar.activation(picked[:, t, :], planes[t][:].indirect(lst[:]), COPY)
            return picked

        def quantize_planes(picked, tag, pieces):
            width = J // pieces
            woven = [sb.tile([P, width, PACK], BF16, name=f"{tag}_woven{h}", tag=f"{tag}_woven{h}", align_bytes=64) for h in range(pieces)]
            codes = [sb.tile([P, width], U32, name=f"{tag}_codes{h}", align_bytes=64) for h in range(pieces)]
            scales = [sb.tile([P, width], U8, name=f"{tag}_scales{h}", align_bytes=64) for h in range(pieces)]
            for step in range(pieces + 1):
                if step < pieces:
                    nc.vector.tensor_copy(
                        woven[step][:].rearrange("p (c i) t -> p c t i", i=4),
                        picked[:, :, step * width : (step + 1) * width].rearrange("p t (c i) -> p c t i", i=4),
                    )
                if step >= 1:
                    h = step - 1
                    nc.vector.quantize_mx(out=codes[h][:].bitcast(FP8X4), scales=scales[h][:], in_=woven[h][:].rearrange("p j t -> p (j t)"))
            return codes, scales

        key_bytes = sb.tile([P, I], U8, name="key_bytes", align_bytes=64)

        def table_chunk(codes, scales, c):
            h, lo = divmod(c * CHUNK, J // len(codes))
            bank = ps_g.tile([P, PACK, CHUNK], F32, name="bank", tag="bank")
            for r in range(PACK):
                nc.tensor.matmul_mx(
                    out=bank[:, r, :],
                    lhsT=key_codes[:, r * P : (r + 1) * P].bitcast(FP8X4),
                    lhsT_scale=key_bytes[:, r * P : (r + 1) * P],
                    rhs=codes[h][:, lo : lo + CHUNK].bitcast(FP8X4),
                    rhs_scale=scales[h][:, lo : lo + CHUNK],
                    start=True,
                    stop=True,
                )
            return bank

        note_picked = gather_planes(note_pl, list_n, "note_picked", (0, 1, 2, 3))
        nc.vector.tensor_copy(key_bytes[:].rearrange("p (r s) -> p s r", r=PACK), key_scales[:].indirect(list_i[:]))
        note_codes, note_scales = quantize_planes(note_picked, "note", 2)
        key_codes = sb.tile([P, I], U32, name="key_codes", tag="note_picked", align_bytes=64)
        nc.vector.tensor_copy(key_codes[:].rearrange("p (r s) -> p s r", r=PACK), key_words[:].indirect(list_i[:]))
        g1_banks = [table_chunk(note_codes, note_scales, c) for c in range(CHUNKS)]

        user_picked = gather_planes(user_pl, list_u, "note_woven1", (1, 2, 3))
        g1_first = sb.tile([P, CHUNK, PACK], F32, name="g1_first", tag="user_pl2")
        g1_rest = sb.tile([P, CHUNKS - 1, CHUNK, PACK], F32, name="g1_rest", tag="user_pl3")
        g1 = [g1_first[:]] + [g1_rest[:, c] for c in range(CHUNKS - 1)]
        nc.scalar.copy(g1[0], g1_banks[0][:].rearrange("p r j -> p j r"))
        user_codes, user_scales = quantize_planes(user_picked, "user", CHUNKS)
        for c in range(1, CHUNKS):
            nc.scalar.copy(g1[c], g1_banks[c][:].rearrange("p r j -> p j r"))
        g2_banks = [table_chunk(user_codes, user_scales, c) for c in range(CHUNKS)]


        def gather_values(b, tag):
            picked = sb.tile([P, I], BF16, name="val_picked", tag=tag, align_bytes=64)
            nc.scalar.activation(picked[:], val_bl[b][:].indirect(list_i[:]), COPY)
            return picked

        def gather_values_shared(b, tag):
            picked = sb.tile([P, I], BF16, name="val_picked", tag=tag, align_bytes=64)
            nc.vector.tensor_copy(picked[:, :HALF], val_bl[b][:].indirect(half_list(list_i, 0)))
            nc.scalar.activation(picked[:, HALF:], val_bl[b][:].indirect(half_list(list_i, 1)), COPY)
            return picked

        def turn_values(b, picked):
            words = picked[:].bitcast(F32)
            turned = ps_g.tile([P, 2, P], F32, name="turned", tag="bank")
            for u in range(2):
                nc.tensor.transpose(turned[:, u, :], words[:, u::2], ident[:])
            nc.scalar.copy(vt_woven[b].bitcast(F32), turned[:].rearrange("p u e -> p e u"))

        def quantize_values(woven, codes, name):
            scales = sb.tile([P, P], U8, name=name, align_bytes=64)
            nc.vector.quantize_mx(out=codes.bitcast(FP8X4), scales=scales[:], in_=woven.rearrange("p e t -> p (e t)"))
            return scales

        larger = [sb.tile([P, 2, CHUNK, PACK], F32, name=f"larger{h}") for h in range(2)]
        gr_woven = [sb.tile([P, 2, CHUNK, PACK], BF16, name=f"gr_woven{h}", tag=f"gr_woven{h}", align_bytes=64) for h in range(2)]
        gr_codes = sb.tile([P, J], U32, name="gr_codes", align_bytes=64)
        gr_scales = sb.tile([P, J], U8, name="gr_scales", align_bytes=64)

        def take_larger(c):
            nc.vector.tensor_tensor(larger[c // 2][:, c % 2], g2_banks[c][:].rearrange("p r j -> p j r"), g1[c], MAX)

        def quantize_table(h):
            cols = slice(h * HALF, (h + 1) * HALF)
            nc.vector.quantize_mx(out=gr_codes[:, cols].bitcast(FP8X4), scales=gr_scales[:, cols], in_=gr_woven[h][:].rearrange("p c j r -> p (c j r)"))

        def finish_block(b, codes, scales, parts):
            width = J // parts
            for part in range(parts):
                cols = slice(part * width, (part + 1) * width)
                sums = ps_o.tile([P, width], F32, name="sums", tag="sums")
                nc.tensor.matmul_mx(
                    out=sums[:],
                    lhsT=codes.bitcast(FP8X4),
                    lhsT_scale=scales,
                    rhs=gr_codes[:, cols].bitcast(FP8X4),
                    rhs_scale=gr_scales[:, cols],
                    start=True,
                    stop=True,
                )
                runs = slice(part * width // RUN, (part + 1) * width // RUN)
                nc.vector.tensor_reduce(best[:, b, runs], sums[:].rearrange("p (n k) -> p n k", k=RUN), AXIS_X, MAX)

        picked = [gather_values(0, "note_woven1"), gather_values(1, "val_picked1")]
        third_picked = gather_values(2, "val_picked2")
        first_woven = [sb.tile([P, P, PACK], BF16, name="first_woven", tag=f"val_bl{b + 1}", align_bytes=64) for b in range(2)]
        later_woven = [sb.tile([P, P, PACK], BF16, name=f"later_woven{b}", align_bytes=64) for b in range(2)]
        vt_woven = [first_woven[0][:], first_woven[1][:], later_woven[0][:], later_woven[1][:]]
        for c in range(CHUNKS):
            take_larger(c)
        for c in range(2):
            nc.gpsimd.tensor_tensor(gr_woven[0][:, c], larger[0][:, c], factor[:, :PACK].unsqueeze(1).to_broadcast([P, CHUNK, PACK]), MULT)
        nc.vector.tensor_tensor(
            gr_woven[1][:].rearrange("p c j r -> p (c j) r"),
            larger[1][:].rearrange("p c j r -> p (c j) r"),
            factor_ps[:, :PACK].unsqueeze(1).to_broadcast([P, HALF, PACK]),
            MULT,
        )
        for h in range(2):
            quantize_table(h)
        turn_values(0, picked[0])
        turn_values(1, picked[1])
        turn_values(2, third_picked)
        first_codes = sb.tile([P, 2, P], U32, name="first_codes", tag="val_picked2", align_bytes=64)
        first_scales = [quantize_values(vt_woven[b], first_codes[:, b], f"first_scales{b}") for b in range(2)]
        last_picked = gather_values_shared(3, "gr_woven1")
        codes = tail.tile([P, P], U32, name="third_codes", align_bytes=64, offset=0)
        scales = quantize_values(vt_woven[2], codes[:], "third_scales")
        best = tail.tile([P, E // P, N], F32, name="best", align_bytes=64, offset=1024)
        out_v = out.rearrange("(b p) n -> p b n", p=P)
        turn_values(3, last_picked)
        finish_block(0, first_codes[:, 0], first_scales[0][:], 1)
        finish_block(1, first_codes[:, 1], first_scales[1][:], 1)
        last_codes = sb.tile([P, P], U32, name="last_codes", align_bytes=64)
        last_scales = quantize_values(vt_woven[3], last_codes[:], "last_scales")
        finish_block(2, codes[:], scales[:], 1)
        nc.sync.dma_start(out_v[:, :3, :], best[:, :3, :])
        finish_block(3, last_codes[:], last_scales[:], 2)
        nc.sync.dma_start(out_v[:, 3, :], best[:, 3, :])
